import numpy as np
import ml_dtypes


def mxq(x, axis, fmt="e4m3"):
    dtype, down = {"e4m3": (ml_dtypes.float8_e4m3fn, 7), "e5m2": (ml_dtypes.float8_e5m2, 14)}[fmt]
    v = np.moveaxis(np.asarray(x, np.float32).astype(ml_dtypes.bfloat16).astype(np.float64), axis, -1)
    blocks = v.reshape(v.shape[:-1] + (-1, 32))
    amax = np.abs(blocks).max(-1, keepdims=True)
    byte = np.maximum(np.where(amax > 0, np.frexp(amax)[1] - 1 + 127, 0) - down, 1)
    scale = np.exp2(byte - 127.0)
    codes = (blocks / scale).astype(np.float32).astype(dtype).astype(np.float64)
    return np.moveaxis((codes * scale).reshape(v.shape), -1, axis)


WIDE = False


def mx_kscale(k):
    if not WIDE:
        return np.ones(k)
    levels = np.array([10, -10, 5, -5, 0])
    if k % 512:
        return np.exp2(np.random.permutation(np.resize(levels, k // 32))).repeat(32)
    a = np.empty((k // 512, 16))
    for p in range(k // 512):
        a[p, :8] = np.random.permutation(np.resize(levels, 8))
        for g in range(8):
            far = levels[np.abs(levels - a[p, g]) >= 10]
            a[p, g + 8] = far[np.random.randint(len(far))]
    return np.exp2(a.ravel()).repeat(32)


def f64(x):
    return np.asarray(x).astype(np.float64)


def striped(idx):
    return np.tile(idx.reshape(-1, 16).T, (8, 1)).astype(np.uint16)


def unstriped(offs):
    return offs[:16].T.reshape(-1).astype(np.int64)


E2M1 = np.array([0.0, 0.5, 1.0, 1.5, 2.0, 3.0, 4.0, 6.0, -0.0, -0.5, -1.0, -1.5, -2.0, -3.0, -4.0, -6.0])


def pack_weight(w, fmt):
    k, n = w.shape
    w = f64(np.asarray(w, np.float32).astype(ml_dtypes.bfloat16)).reshape(k // 32, 32, n)
    amax = np.abs(w).max(1)
    if fmt == "e4m3":
        byte = np.frexp(amax)[1] - 1 + 127 - 7
    else:
        mant, ex = np.frexp(amax / 6.0)
        byte = np.where(mant > 0.5, ex, ex - 1) + 127
    byte = np.clip(np.where(amax > 0, byte, 1), 1, 254)
    scaled = (w * np.exp2(127.0 - byte)[:, None, :]).reshape(k, n).astype(np.float32)
    by_word = np.ascontiguousarray(scaled.reshape(k // 512, 128, 4, n).transpose(0, 1, 3, 2))
    if fmt == "e4m3":
        words = by_word.astype(ml_dtypes.float8_e4m3fn).view(np.uint8)
    else:
        c = by_word.astype(ml_dtypes.float4_e2m1fn).view(np.uint8) & 0xF
        words = (c[..., 0::2] | (c[..., 1::2] << 4)).reshape(k // 512, 128, 2 * n)
    return np.ascontiguousarray(words), np.ascontiguousarray(byte.astype(np.uint8).reshape(k // 512, 16, n))


def unpack_weight(words, scales, fmt):
    g, _, n = scales.shape
    words = np.ascontiguousarray(words).reshape(g, 128, n, -1)
    if fmt == "e4m3":
        vals = words.view(ml_dtypes.float8_e4m3fn).astype(np.float64)
    else:
        nib = np.empty((g, 128, n, 4), np.uint8)
        nib[..., 0::2] = words & 0xF
        nib[..., 1::2] = words >> 4
        vals = E2M1[nib]
    vals = vals * np.repeat(np.exp2(scales.astype(np.float64) - 127.0), 8, axis=1)[..., None]
    return vals.transpose(0, 1, 3, 2).reshape(g * 512, n)


def gelu(v):
    return 0.5 * v * (1.0 + np.tanh(np.sqrt(2.0 / np.pi) * (v + 0.044715 * v**3)))


K, T, S, H, N, P, P2 = 1024, 4096, 2048, 1024, 768, 1024, 512


def setup_inputs():
    n = np.random.standard_normal
    s = mx_kscale(K)[:, None]
    u = mx_kscale(H)[:, None]
    tab_words, tab_scales = pack_weight(n((K, T)) * s, "e4m3")
    w4_words, w4_scales = pack_weight(n((H, N)) / np.sqrt(H) / u, "e2m1")
    return {
        "tab_words": tab_words,
        "tab_scales": tab_scales,
        "offs": striped(np.random.permutation(T)[:S]),
        "pos1": striped(np.random.permutation(S)[:P]),
        "pos2": striped(np.random.permutation(S)[:P]),
        "pos3": striped(np.random.permutation(P)[:P2]),
        "pos4": striped(np.random.permutation(S)[:P2]),
        "w1": (1.5 * n((K, H)) / np.sqrt(K) / s).astype(np.float32),
        "gain": (np.exp(0.4 * n(H)) * u[:, 0]).astype(np.float32),
        "w4_words": w4_words,
        "w4_scales": w4_scales,
        "w5": (n((H, N)) / np.sqrt(H) / u).astype(np.float32),
    }


def reference(tab_words, tab_scales, offs, pos1, pos2, pos3, pos4, w1, gain,
              w4_words, w4_scales, w5):
    v = unpack_weight(tab_words, tab_scales, "e4m3")[:, unstriped(offs)]
    h = mxq(f64(w1), 0, "e4m3").T @ v
    a1 = np.maximum(h[:, unstriped(pos1)], h[:, unstriped(pos2)])
    both = a1[:, unstriped(pos3)] + np.tanh(h[:, unstriped(pos4)])
    a2 = mxq(f64(gain)[:, None] * both, 0, "e4m3")
    w4 = unpack_weight(w4_words, w4_scales, "e2m1")
    e1 = w4.T @ a2
    e2 = mxq(f64(w5), 0, "e4m3").T @ a2
    return np.maximum(e1, e2)

@@ -1,0 +1,267 @@
+from contextlib import ExitStack
+
+import concourse.mybir as mybir
+
+K, T, S, H, N, PAIRS, KEPT = 1024, 4096, 2048, 1024, 768, 1024, 512
+FLOPS = 2 * K * H * S + 2 * 2 * H * N * KEPT
+
+F32 = mybir.dt.float32
+BF16 = mybir.dt.bfloat16
+I32 = mybir.dt.int32
+U32 = mybir.dt.uint32
+U16 = mybir.dt.uint16
+U8 = mybir.dt.uint8
+FP8X4 = mybir.dt.float8_e4m3fn_x4
+FP4X4 = mybir.dt.float4_e2m1fn_x4
+ACT = mybir.ActivationFunctionType
+ALU = mybir.AluOpType
+
+P = 128
+PACK = 4
+K_PASS = P * PACK
+BANK = 512
+W5_PIECE = 384
+TAIL = 128
+TILES_PER_BANK = 3
+
+
+def tile_list_gravestone_inscription_scores_kernel(
+    tc, tab_words, tab_scales, offs, pos1, pos2, pos3, pos4, w1, gain, w4_words, w4_scales, w5, out
+):
+    nc = tc.nc
+    with ExitStack() as ctx:
+        keep = ctx.enter_context(tc.tile_pool(name="keep", bufs=1))
+        ring = ctx.enter_context(tc.tile_pool(name="ring", bufs=2))
+        psum = ctx.enter_context(tc.psum_pool(name="psum", bufs=8))
+
+        def load_list(src, name):
+            t = keep.tile(list(src.shape), U16, name=name)
+            nc.sync.dma_start(t[:], src)
+            return t
+
+        offs_sb = load_list(offs, "offs_sb")
+        pos1_sb = load_list(pos1, "pos1_sb")
+        pos2_sb = load_list(pos2, "pos2_sb")
+        scale_rows = keep.tile([P, T], U8, name="scale_rows", align_bytes=64)
+        nc.vector.memset(scale_rows[:].bitcast(I32), 0)
+        for q in range(4):
+            nc.sync.dma_start(
+                scale_rows[32 * q : 32 * q + 8, :].bitcast(I32),
+                tab_scales[:, 4 * q : 4 * q + 4, :].bitcast(I32),
+            )
+        words = []
+        for a in range(2):
+            t = keep.tile([P, T], U32, name="words%d" % a, align_bytes=64)
+            nc.sync.dma_start(t[:].bitcast(I32), tab_words[a].rearrange("p t i -> p (t i)").bitcast(I32))
+            words.append(t)
+
+        def load_rows(w, a, c0, width):
+            raw = ring.tile([P, PACK, width], F32, name="raw", bufs=4)
+            nc.sync.dma_start(
+                raw[:], w[a * K_PASS : (a + 1) * K_PASS, c0 : c0 + width].rearrange("(p j) c -> p j c", j=PACK)
+            )
+            return raw
+
+        w1_raw = {}
+        for a in range(2):
+            w1_raw[a, 0] = load_rows(w1, a, 0, K_PASS)
+        pos4_sb = load_list(pos4, "pos4_sb")
+        pos3_sb = load_list(pos3, "pos3_sb")
+        gain_sb = keep.tile([P, 2, PACK], F32, name="gain_sb")
+        nc.sync.dma_start(gain_sb[:], gain.rearrange("(b p t) -> p b t", b=2, t=PACK))
+        for a in range(2):
+            w1_raw[a, 1] = load_rows(w1, a, K_PASS, K_PASS)
+
+        picked_scales = keep.tile([P, S], U8, name="picked_scales", align_bytes=64)
+        nc.vector.tensor_copy(picked_scales[:], scale_rows[:].indirect(offs_sb[:]))
+        picked_low = keep.tile([P, S], U32, name="picked_low", align_bytes=64)
+        nc.vector.tensor_copy(picked_low[:], words[0][:].indirect(offs_sb[:]))
+        picked = [[picked_low[:, c * BANK : (c + 1) * BANK] for c in range(S // BANK)], []]
+
+        def pick_high(c, tag):
+            t = keep.tile([P, BANK], U32, name="picked_high%d" % c, tag=tag, align_bytes=64)
+            nc.vector.tensor_copy(t[:], words[1][:].indirect(offs_sb[:, c * BANK // 16 : (c + 1) * BANK // 16]))
+            picked[1].append(t[:])
+
+        w1_codes, w1_planes = {}, {}
+
+        for a in range(2):
+            for b in range(2):
+                w1_codes[a, b] = keep.tile([P, K_PASS], U32, name="w1_codes%d%d" % (a, b), align_bytes=64)
+                w1_planes[a, b] = keep.tile([P, K_PASS], U8, name="w1_planes%d%d" % (a, b), align_bytes=64)
+
+        def quantise_w1(a, b, t0, t1, rounded=None):
+            if rounded is None:
+                rounded = ring.tile([P, t1 - t0, P, PACK], BF16, name="rounded", align_bytes=64, bufs=3)
+            nc.scalar.copy(
+                rounded[:].rearrange("p t m j -> p m j t"),
+                w1_raw[a, b][:].rearrange("p j (m t) -> p m j t", t=PACK)[:, :, :, t0:t1],
+            )
+            nc.vector.quantize_mx(
+                out=w1_codes[a, b][:, t0 * P : t1 * P].bitcast(FP8X4),
+                scales=w1_planes[a, b][:, t0 * P : t1 * P],
+                in_=rounded[:].rearrange("p t m j -> p (t m j)"),
+            )
+
+        w5_codes = [keep.tile([P, N], U32, name="w5_codes%d" % a, align_bytes=64) for a in range(2)]
+        w5_planes = [keep.tile([P, N], U8, name="w5_planes%d" % a, align_bytes=64) for a in range(2)]
+
+        def quantise_w5(a, c0):
+            raw = load_rows(w5, a, c0, W5_PIECE)
+            rounded = ring.tile([P, W5_PIECE, PACK], BF16, name="rounded", align_bytes=64, bufs=3)
+            nc.scalar.copy(
+                rounded[:].rearrange("p (c i) j -> p c j i", i=4),
+                raw[:].rearrange("p j (c i) -> p c j i", i=4),
+            )
+            nc.vector.quantize_mx(
+                out=w5_codes[a][:, c0 : c0 + W5_PIECE].bitcast(FP8X4),
+                scales=w5_planes[a][:, c0 : c0 + W5_PIECE],
+                in_=rounded[:].rearrange("p c j -> p (c j)"),
+            )
+
+        def features(b, t):
+            h = ring.tile([P, S], F32, name="h", bufs=3)
+            m = slice(t * P, (t + 1) * P)
+            for c in range(S // BANK):
+                cols = slice(c * BANK, (c + 1) * BANK)
+                acc = psum.tile([P, BANK], F32, name="bank")
+                for a in range(2):
+                    nc.tensor.matmul_mx(
+                        out=acc[:],
+                        lhsT=w1_codes[a, b][:, m].bitcast(FP8X4),
+                        lhsT_scale=w1_planes[a, b][:, m],
+                        rhs=picked[a][c].bitcast(FP8X4),
+                        rhs_scale=picked_scales[4 * a : P, cols],
+                        start=(a == 0),
+                        stop=(a == 1),
+                    )
+                if (b, t) == (0, 0):
+                    nc.vector.tensor_copy(h[:, cols], acc[:])
+                else:
+                    nc.scalar.copy(h[:, cols], acc[:])
+            return h
+
+        def pairs(h):
+            first = ring.tile([P, PAIRS], F32, name="first")
+            second = ring.tile([P, PAIRS], F32, name="second")
+            entry = ring.tile([P, KEPT], F32, name="entry")
+            nc.vector.tensor_copy(first[:], h[:].indirect(pos1_sb[:]))
+            nc.vector.tensor_copy(second[:], h[:].indirect(pos2_sb[:]))
+            nc.vector.tensor_copy(entry[:], h[:].indirect(pos4_sb[:]))
+            a1 = ring.tile([P, PAIRS], F32, name="a1", bufs=4)
+            nc.vector.tensor_tensor(a1[:], first[:], second[:], ALU.max)
+            bounded = ring.tile([P, KEPT], F32, name="bounded", bufs=4)
+            nc.scalar.activation(bounded[:], entry[:], ACT.Tanh)
+            return a1, bounded
+
+        def kept(a1, bounded, b, t, j0, width, a2):
+            both = ring.tile([P, width], F32, name="both", bufs=4)
+            nc.vector.tensor_tensor(
+                both[:], a1[:].indirect(pos3_sb[:, j0 // 16 : (j0 + width) // 16]), bounded[:, j0 : j0 + width], ALU.add
+            )
+            nc.scalar.activation(a2[:, :, t], both[:], ACT.Copy, scale=gain_sb[:, b, t : t + 1])
+
+        def quantise_a2(a2, width, name):
+            codes = keep.tile([P, width], U32, name=name + "_codes", align_bytes=64)
+            plane = keep.tile([P, width], U8, name=name + "_plane", align_bytes=64)
+            nc.vector.quantize_mx(out=codes[:].bitcast(FP8X4), scales=plane[:], in_=a2[:].rearrange("p j t -> p (j t)"))
+            return codes, plane
+
+        pick_high(0, "picked_high0")
+        pick_high(1, "picked_high1")
+        quantise_w1(0, 0, 0, 1, keep.tile([P, 1, P, PACK], BF16, name="first_rounded", tag="picked_high2", align_bytes=64))
+        pick_high(2, "picked_high2")
+        pick_high(3, "picked_high3")
+        quantise_w1(1, 0, 0, 1)
+
+        w4_sb = keep.tile([P, 2, 2 * N], U8, name="w4_sb", align_bytes=64)
+        w4_planes = keep.tile([P, 2, N], U8, name="w4_planes", align_bytes=64)
+
+        a2_low = keep.tile([P, KEPT, PACK], BF16, name="a2_low", align_bytes=64)
+        waiting = None
+        for t in range(PACK):
+            h = features(0, t)
+            if t == 0:
+                quantise_w1(0, 0, 1, PACK)
+                quantise_w1(1, 0, 1, PACK)
+            made = pairs(h)
+            if waiting is not None:
+                kept(*waiting, 0, t - 1, 0, KEPT, a2_low)
+            waiting = made
+            if t < 2:
+                quantise_w1(t, 1, 0, PACK)
+            if t == 1:
+                nc.sync.dma_start(w4_sb[:].bitcast(I32), w4_words.rearrange("a p c -> p a c").bitcast(I32))
+                nc.gpsimd.memset(w4_planes[:].bitcast(I32), 0)
+                for q in range(4):
+                    nc.sync.dma_start(
+                        w4_planes[32 * q : 32 * q + 4, :, :].bitcast(I32),
+                        w4_scales[:, 4 * q : 4 * q + 4, :].rearrange("a r c -> r a c").bitcast(I32),
+                    )
+        high = []
+        for t in range(PACK):
+            h = features(1, t)
+            high.append(pairs(h))
+            if t == 0:
+                kept(*waiting, 0, PACK - 1, 0, KEPT, a2_low)
+            if t == 1:
+                low_codes, low_plane = quantise_a2(a2_low, KEPT, "low")
+            quantise_w5(t // 2, (t % 2) * W5_PIECE)
+
+        def scores(j0, a2_high):
+            high_codes, high_plane = quantise_a2(a2_high, TAIL, "high%d" % j0)
+            moving = [
+                (low_codes[:, j0 : j0 + TAIL], low_plane[:, j0 : j0 + TAIL]),
+                (high_codes[:], high_plane[:]),
+            ]
+            banks = {}
+            for n0 in range(0, N // P, TILES_PER_BANK):
+                for which in range(2):
+                    banks[n0, which] = psum.tile([P, TILES_PER_BANK, TAIL], F32, name="bank")
+            for a in range(2):
+                for n0 in range(0, N // P, TILES_PER_BANK):
+                    for which in range(2):
+                        for i in range(TILES_PER_BANK):
+                            n = slice((n0 + i) * P, (n0 + i + 1) * P)
+                            if which == 0:
+                                lhsT = w4_sb[:, a, 2 * n.start : 2 * n.stop].bitcast(FP4X4)
+                                lhsT_scale = w4_planes[:, a, n]
+                            else:
+                                lhsT = w5_codes[a][:, n].bitcast(FP8X4)
+                                lhsT_scale = w5_planes[a][:, n]
+                            nc.tensor.matmul_mx(
+                                out=banks[n0, which][:, i, :],
+                                lhsT=lhsT,
+                                lhsT_scale=lhsT_scale,
+                                rhs=moving[a][0].bitcast(FP8X4),
+                                rhs_scale=moving[a][1],
+                                start=(a == 0 and i == 0),
+                                stop=(a == 1 and i == TILES_PER_BANK - 1),
+                            )
+            return banks
+
+        def higher(j0, banks):
+            for n0 in range(0, N // P, TILES_PER_BANK):
+                e1 = ring.tile([P, TILES_PER_BANK, TAIL], F32, name="e1")
+                nc.scalar.copy(e1[:], banks[n0, 0][:])
+                best = ring.tile([P, TILES_PER_BANK, TAIL], F32, name="best", bufs=4)
+                nc.vector.tensor_tensor(best[:], banks[n0, 1][:], e1[:], ALU.max)
+                nc.sync.dma_start(
+                    out[n0 * P : (n0 + TILES_PER_BANK) * P, j0 : j0 + TAIL].rearrange("(i p) j -> p i j", p=P),
+                    best[:],
+                )
+
+        chunks = list(range(0, KEPT, TAIL))
+        rounded_a2, open_banks = {}, {}
+        for step in range(len(chunks) + 2):
+            if step < len(chunks):
+                j0 = chunks[step]
+                rounded_a2[j0] = ring.tile([P, TAIL, PACK], BF16, name="a2_high", align_bytes=64, bufs=4)
+                for t in range(PACK):
+                    kept(*high[t], 1, t, j0, TAIL, rounded_a2[j0])
+            if 1 <= step <= len(chunks):
+                j0 = chunks[step - 1]
+                open_banks[j0] = scores(j0, rounded_a2[j0])
+            if step >= 2:
+                j0 = chunks[step - 2]
+                higher(j0, open_banks[j0])

@@ -20,9 +20,15 @@ P = 128
 PACK = 4
 K_PASS = P * PACK
 BANK = 512
+SLICES = H // P
+AHEAD = 3
 W5_PIECE = 384
-TAIL = 128
-TILES_PER_BANK = 3
+CHUNK = 128
+BANK_SUMS = (
+    ((0, 0), (0, 1), (0, 2), (0, 3)),
+    ((1, 0), (1, 1), (1, 2), (1, 3)),
+    ((0, 4), (0, 5), (1, 4), (1, 5)),
+)
 
 
 def tile_list_gravestone_inscription_scores_kernel(
@@ -34,65 +40,72 @@ def tile_list_gravestone_inscription_scores_kernel(
         ring = ctx.enter_context(tc.tile_pool(name="ring", bufs=2))
         psum = ctx.enter_context(tc.psum_pool(name="psum", bufs=8))
 
+        def mx_tile(shape, dtype, name, tag=None):
+            return keep.tile(shape, dtype, name=name, tag=tag or name, align_bytes=64)
+
         def load_list(src, name):
             t = keep.tile(list(src.shape), U16, name=name)
             nc.sync.dma_start(t[:], src)
             return t
 
-        offs_sb = load_list(offs, "offs_sb")
-        pos1_sb = load_list(pos1, "pos1_sb")
-        pos2_sb = load_list(pos2, "pos2_sb")
-        scale_rows = keep.tile([P, T], U8, name="scale_rows", align_bytes=64)
-        nc.vector.memset(scale_rows[:].bitcast(I32), 0)
-        for q in range(4):
-            nc.sync.dma_start(
-                scale_rows[32 * q : 32 * q + 8, :].bitcast(I32),
-                tab_scales[:, 4 * q : 4 * q + 4, :].bitcast(I32),
-            )
-        words = []
-        for a in range(2):
-            t = keep.tile([P, T], U32, name="words%d" % a, align_bytes=64)
-            nc.sync.dma_start(t[:].bitcast(I32), tab_words[a].rearrange("p t i -> p (t i)").bitcast(I32))
-            words.append(t)
-
-        def load_rows(w, a, c0, width):
-            raw = ring.tile([P, PACK, width], F32, name="raw", bufs=4)
+        def load_rows(w, a, c0, width, name, tag):
+            raw = mx_tile([P, PACK, width], F32, name, tag)
             nc.sync.dma_start(
                 raw[:], w[a * K_PASS : (a + 1) * K_PASS, c0 : c0 + width].rearrange("(p j) c -> p j c", j=PACK)
             )
             return raw
 
+        def entries(lst, j0, count):
+            return lst[:, j0 // 16 : (j0 + count) // 16]
+
+        offs_sb = load_list(offs, "offs_sb")
+        scale_rows = mx_tile([P, T], U8, "scale_rows")
+        nc.sync.dma_start(
+            scale_rows[:].bitcast(I32),
+            tab_scales.rearrange("a q t -> (a q) t").bitcast(I32).unsqueeze(1).to_broadcast([32, 4, T // 4]),
+        )
+        pos4_sb = load_list(pos4, "pos4_sb")
+        pos1_sb = load_list(pos1, "pos1_sb")
+        pos2_sb = load_list(pos2, "pos2_sb")
+        pos3_sb = load_list(pos3, "pos3_sb")
+        words = []
+        for a in range(2):
+            t = mx_tile([P, T], U32, "words%d" % a)
+            nc.sync.dma_start(t[:].bitcast(I32), tab_words[a].rearrange("p t i -> p (t i)").bitcast(I32))
+            words.append(t)
         w1_raw = {}
         for a in range(2):
-            w1_raw[a, 0] = load_rows(w1, a, 0, K_PASS)
-        pos4_sb = load_list(pos4, "pos4_sb")
-        pos3_sb = load_list(pos3, "pos3_sb")
+            w1_raw[a, 0] = load_rows(w1, a, 0, K_PASS, "w1_raw%d0" % a, ("raw_even", "raw_odd")[a])
         gain_sb = keep.tile([P, 2, PACK], F32, name="gain_sb")
         nc.sync.dma_start(gain_sb[:], gain.rearrange("(b p t) -> p b t", b=2, t=PACK))
-        for a in range(2):
-            w1_raw[a, 1] = load_rows(w1, a, K_PASS, K_PASS)
 
-        picked_scales = keep.tile([P, S], U8, name="picked_scales", align_bytes=64)
-        nc.vector.tensor_copy(picked_scales[:], scale_rows[:].indirect(offs_sb[:]))
-        picked_low = keep.tile([P, S], U32, name="picked_low", align_bytes=64)
+        picked_rows = mx_tile([P, S], U8, "picked_rows")
+        nc.vector.tensor_copy(picked_rows[:], scale_rows[:].indirect(offs_sb[:]))
+        picked_scales = [mx_tile([P, S], U8, "picked_scales%d" % a) for a in range(2)]
+        for a in range(2):
+            nc.gpsimd.memset(picked_scales[a][:].bitcast(I32), 0)
+            for q in range(4):
+                row = 16 * a + 4 * q
+                (nc.scalar, nc.sync)[a].dma_start(
+                    picked_scales[a][32 * q : 32 * q + 4, :].bitcast(I32),
+                    picked_rows[4 * row : 4 * row + 16 : 4, :].bitcast(I32),
+                )
+        picked_low = mx_tile([P, S], U32, "picked_low")
         nc.vector.tensor_copy(picked_low[:], words[0][:].indirect(offs_sb[:]))
         picked = [[picked_low[:, c * BANK : (c + 1) * BANK] for c in range(S // BANK)], []]
 
-        def pick_high(c, tag):
-            t = keep.tile([P, BANK], U32, name="picked_high%d" % c, tag=tag, align_bytes=64)
-            nc.vector.tensor_copy(t[:], words[1][:].indirect(offs_sb[:, c * BANK // 16 : (c + 1) * BANK // 16]))
+        def pick_high(c):
+            t = mx_tile([P, BANK], U32, "picked_high%d" % c)
+            nc.vector.tensor_copy(t[:], words[1][:].indirect(entries(offs_sb, c * BANK, BANK)))
             picked[1].append(t[:])
 
         w1_codes, w1_planes = {}, {}
-
         for a in range(2):
             for b in range(2):
-                w1_codes[a, b] = keep.tile([P, K_PASS], U32, name="w1_codes%d%d" % (a, b), align_bytes=64)
-                w1_planes[a, b] = keep.tile([P, K_PASS], U8, name="w1_planes%d%d" % (a, b), align_bytes=64)
+                w1_codes[a, b] = mx_tile([P, K_PASS], U32, "w1_codes%d%d" % (a, b))
+                w1_planes[a, b] = mx_tile([P, K_PASS], U8, "w1_planes%d%d" % (a, b))
 
-        def quantise_w1(a, b, t0, t1, rounded=None):
-            if rounded is None:
-                rounded = ring.tile([P, t1 - t0, P, PACK], BF16, name="rounded", align_bytes=64, bufs=3)
+        def quantise_w1(a, b, t0, t1, rounded):
             nc.scalar.copy(
                 rounded[:].rearrange("p t m j -> p m j t"),
                 w1_raw[a, b][:].rearrange("p j (m t) -> p m j t", t=PACK)[:, :, :, t0:t1],
@@ -103,15 +116,17 @@ def tile_list_gravestone_inscription_scores_kernel(
                 in_=rounded[:].rearrange("p t m j -> p (t m j)"),
             )
 
-        w5_codes = [keep.tile([P, N], U32, name="w5_codes%d" % a, align_bytes=64) for a in range(2)]
-        w5_planes = [keep.tile([P, N], U8, name="w5_planes%d" % a, align_bytes=64) for a in range(2)]
+        def rounded_tile(shape):
+            return ring.tile(shape, BF16, name="rounded", align_bytes=64)
+
+        w5_codes = [mx_tile([P, N], U32, "w5_codes%d" % a) for a in range(2)]
+        w5_planes = [mx_tile([P, N], U8, "w5_planes%d" % a) for a in range(2)]
 
         def quantise_w5(a, c0):
-            raw = load_rows(w5, a, c0, W5_PIECE)
-            rounded = ring.tile([P, W5_PIECE, PACK], BF16, name="rounded", align_bytes=64, bufs=3)
+            rounded = rounded_tile([P, W5_PIECE, PACK])
             nc.scalar.copy(
                 rounded[:].rearrange("p (c i) j -> p c j i", i=4),
-                raw[:].rearrange("p j (c i) -> p c j i", i=4),
+                w5_raw[a][:, :, c0 : c0 + W5_PIECE].rearrange("p j (c i) -> p c j i", i=4),
             )
             nc.vector.quantize_mx(
                 out=w5_codes[a][:, c0 : c0 + W5_PIECE].bitcast(FP8X4),
@@ -119,8 +134,9 @@ def tile_list_gravestone_inscription_scores_kernel(
                 in_=rounded[:].rearrange("p c j -> p (c j)"),
             )
 
-        def features(b, t):
-            h = ring.tile([P, S], F32, name="h", bufs=3)
+        def features(s):
+            b, t = divmod(s, PACK)
+            h = ring.tile([P, S], F32, name="h", bufs=AHEAD)
             m = slice(t * P, (t + 1) * P)
             for c in range(S // BANK):
                 cols = slice(c * BANK, (c + 1) * BANK)
@@ -131,137 +147,151 @@ def tile_list_gravestone_inscription_scores_kernel(
                         lhsT=w1_codes[a, b][:, m].bitcast(FP8X4),
                         lhsT_scale=w1_planes[a, b][:, m],
                         rhs=picked[a][c].bitcast(FP8X4),
-                        rhs_scale=picked_scales[4 * a : P, cols],
+                        rhs_scale=picked_scales[a][:, cols],
                         start=(a == 0),
                         stop=(a == 1),
                     )
-                if (b, t) == (0, 0):
+                if s == 0:
                     nc.vector.tensor_copy(h[:, cols], acc[:])
                 else:
                     nc.scalar.copy(h[:, cols], acc[:])
             return h
 
-        def pairs(h):
-            first = ring.tile([P, PAIRS], F32, name="first")
-            second = ring.tile([P, PAIRS], F32, name="second")
-            entry = ring.tile([P, KEPT], F32, name="entry")
-            nc.vector.tensor_copy(first[:], h[:].indirect(pos1_sb[:]))
-            nc.vector.tensor_copy(second[:], h[:].indirect(pos2_sb[:]))
-            nc.vector.tensor_copy(entry[:], h[:].indirect(pos4_sb[:]))
-            a1 = ring.tile([P, PAIRS], F32, name="a1", bufs=4)
-            nc.vector.tensor_tensor(a1[:], first[:], second[:], ALU.max)
-            bounded = ring.tile([P, KEPT], F32, name="bounded", bufs=4)
-            nc.scalar.activation(bounded[:], entry[:], ACT.Tanh)
-            return a1, bounded
-
-        def kept(a1, bounded, b, t, j0, width, a2):
-            both = ring.tile([P, width], F32, name="both", bufs=4)
+        def kept_sum(s, j0, width, both):
             nc.vector.tensor_tensor(
-                both[:], a1[:].indirect(pos3_sb[:, j0 // 16 : (j0 + width) // 16]), bounded[:, j0 : j0 + width], ALU.add
+                both, a1[s][:].indirect(entries(pos3_sb, j0, width)), bounded[s][:, j0 : j0 + width], ALU.add
             )
-            nc.scalar.activation(a2[:, :, t], both[:], ACT.Copy, scale=gain_sb[:, b, t : t + 1])
+
+        def round_a2(s, both, a2):
+            b, t = divmod(s, PACK)
+            nc.scalar.activation(a2[:, :, t], both, ACT.Copy, scale=gain_sb[:, b, t : t + 1])
 
         def quantise_a2(a2, width, name):
-            codes = keep.tile([P, width], U32, name=name + "_codes", align_bytes=64)
-            plane = keep.tile([P, width], U8, name=name + "_plane", align_bytes=64)
+            codes = mx_tile([P, width], U32, name + "_codes")
+            plane = mx_tile([P, width], U8, name + "_plane")
             nc.vector.quantize_mx(out=codes[:].bitcast(FP8X4), scales=plane[:], in_=a2[:].rearrange("p j t -> p (j t)"))
             return codes, plane
 
-        pick_high(0, "picked_high0")
-        pick_high(1, "picked_high1")
-        quantise_w1(0, 0, 0, 1, keep.tile([P, 1, P, PACK], BF16, name="first_rounded", tag="picked_high2", align_bytes=64))
-        pick_high(2, "picked_high2")
-        pick_high(3, "picked_high3")
-        quantise_w1(1, 0, 0, 1)
+        pick_high(0)
+        pick_high(1)
+        quantise_w1(0, 0, 0, 1, mx_tile([P, 1, P, PACK], BF16, "first_rounded", "picked_high2"))
+        pick_high(2)
+        pick_high(3)
+        quantise_w1(1, 0, 0, 1, mx_tile([P, 1, P, PACK], BF16, "second_rounded", "w4_planes"))
+        hs = [features(0)]
+        quantise_w1(0, 0, 1, PACK, mx_tile([P, PACK - 1, P, PACK], BF16, "third_rounded", "w4_planes"))
+        quantise_w1(1, 0, 1, PACK, rounded_tile([P, PACK - 1, P, PACK]))
+        for s in range(1, AHEAD):
+            hs.append(features(s))
 
-        w4_sb = keep.tile([P, 2, 2 * N], U8, name="w4_sb", align_bytes=64)
-        w4_planes = keep.tile([P, 2, N], U8, name="w4_planes", align_bytes=64)
+        for a in range(2):
+            w1_raw[a, 1] = load_rows(w1, a, K_PASS, K_PASS, "w1_raw%d1" % a, ("raw_even", "raw_odd")[a])
+        w5_raw = [load_rows(w5, a, 0, N, "w5_raw%d" % a, "words%d" % a) for a in range(2)]
+        w4_sb = mx_tile([P, 2, 2 * N], U8, "w4_sb", "picked_rows")
+        nc.sync.dma_start(w4_sb[:].bitcast(I32), w4_words.rearrange("a p c -> p a c").bitcast(I32))
+        w4_planes = mx_tile([P, 2, N], U8, "w4_planes")
+        nc.gpsimd.memset(w4_planes[:].bitcast(I32), 0)
+        for q in range(4):
+            nc.sync.dma_start(
+                w4_planes[32 * q : 32 * q + 4, :, :].bitcast(I32),
+                w4_scales[:, 4 * q : 4 * q + 4, :].rearrange("a r c -> r a c").bitcast(I32),
+            )
 
-        a2_low = keep.tile([P, KEPT, PACK], BF16, name="a2_low", align_bytes=64)
-        waiting = None
-        for t in range(PACK):
-            h = features(0, t)
-            if t == 0:
-                quantise_w1(0, 0, 1, PACK)
-                quantise_w1(1, 0, 1, PACK)
-            made = pairs(h)
-            if waiting is not None:
-                kept(*waiting, 0, t - 1, 0, KEPT, a2_low)
-            waiting = made
-            if t < 2:
-                quantise_w1(t, 1, 0, PACK)
-            if t == 1:
-                nc.sync.dma_start(w4_sb[:].bitcast(I32), w4_words.rearrange("a p c -> p a c").bitcast(I32))
-                nc.gpsimd.memset(w4_planes[:].bitcast(I32), 0)
-                for q in range(4):
-                    nc.sync.dma_start(
-                        w4_planes[32 * q : 32 * q + 4, :, :].bitcast(I32),
-                        w4_scales[:, 4 * q : 4 * q + 4, :].rearrange("a r c -> r a c").bitcast(I32),
-                    )
-        high = []
-        for t in range(PACK):
-            h = features(1, t)
-            high.append(pairs(h))
-            if t == 0:
-                kept(*waiting, 0, PACK - 1, 0, KEPT, a2_low)
-            if t == 1:
+        a2_low = mx_tile([P, KEPT, PACK], BF16, "a2_low")
+        a2_high = [mx_tile([P, CHUNK, PACK], BF16, "a2_high%d" % c) for c in range(KEPT // CHUNK)]
+        a1, bounded = [], []
+        half = PAIRS // 2
+        for s in range(SLICES):
+            h = hs[s]
+            entry = keep.tile([P, KEPT], F32, name="entry%d" % s, tag="entry%d" % s)
+            nc.vector.tensor_copy(entry[:], h[:].indirect(pos4_sb[:]))
+            bounded.append(ring.tile([P, KEPT], F32, name="bounded", bufs=4))
+            nc.scalar.activation(bounded[s][:], entry[:], ACT.Tanh)
+            first = ring.tile([P, PAIRS], F32, name="first")
+            nc.vector.tensor_copy(first[:], h[:].indirect(pos1_sb[:]))
+            if s > 0:
+                width = KEPT if s <= PACK else CHUNK
+                both = keep.tile([P, width], F32, name="both%d" % s, tag="entry%d" % s)
+                kept_sum(s - 1, 0, width, both[:])
+            second = keep.tile([P, PAIRS], F32, name="second%d" % s, tag="second")
+            for j0 in (0, half):
+                nc.vector.tensor_copy(second[:, j0 : j0 + half], h[:].indirect(entries(pos2_sb, j0, half)))
+            a1.append(ring.tile([P, PAIRS], F32, name="a1", bufs=4))
+            for j0 in (0, half):
+                cols = slice(j0, j0 + half)
+                nc.vector.tensor_tensor(a1[s][:, cols], first[:, cols], second[:, cols], ALU.max)
+            if s < 2:
+                quantise_w1(s, 1, 0, PACK, rounded_tile([P, PACK, P, PACK]))
+            if s > 0:
+                round_a2(s - 1, both[:], a2_low if s <= PACK else a2_high[0])
+            if s + AHEAD < SLICES:
+                hs.append(features(s + AHEAD))
+            if s == PACK + 1:
                 low_codes, low_plane = quantise_a2(a2_low, KEPT, "low")
-            quantise_w5(t // 2, (t % 2) * W5_PIECE)
+            if s in (PACK + 1, PACK + 2):
+                for c0 in range(0, N, W5_PIECE):
+                    quantise_w5(s - PACK - 1, c0)
 
-        def scores(j0, a2_high):
-            high_codes, high_plane = quantise_a2(a2_high, TAIL, "high%d" % j0)
+        late = keep.tile([P, KEPT * PACK], F32, name="late", tag="second")
+
+        def finish_a2(s, c):
+            at = (c * PACK + s - PACK) * CHUNK
+            kept_sum(s, c * CHUNK, CHUNK, late[:, at : at + CHUNK])
+            round_a2(s, late[:, at : at + CHUNK], a2_high[c])
+
+        def scores(c):
+            j0 = c * CHUNK
+            high_codes, high_plane = quantise_a2(a2_high[c], CHUNK, "high%d" % c)
             moving = [
-                (low_codes[:, j0 : j0 + TAIL], low_plane[:, j0 : j0 + TAIL]),
+                (low_codes[:, j0 : j0 + CHUNK], low_plane[:, j0 : j0 + CHUNK]),
                 (high_codes[:], high_plane[:]),
             ]
-            banks = {}
-            for n0 in range(0, N // P, TILES_PER_BANK):
-                for which in range(2):
-                    banks[n0, which] = psum.tile([P, TILES_PER_BANK, TAIL], F32, name="bank")
+            banks = [psum.tile([P, PACK, CHUNK], F32, name="bank") for sums in BANK_SUMS]
             for a in range(2):
-                for n0 in range(0, N // P, TILES_PER_BANK):
-                    for which in range(2):
-                        for i in range(TILES_PER_BANK):
-                            n = slice((n0 + i) * P, (n0 + i + 1) * P)
-                            if which == 0:
-                                lhsT = w4_sb[:, a, 2 * n.start : 2 * n.stop].bitcast(FP4X4)
-                                lhsT_scale = w4_planes[:, a, n]
-                            else:
-                                lhsT = w5_codes[a][:, n].bitcast(FP8X4)
-                                lhsT_scale = w5_planes[a][:, n]
-                            nc.tensor.matmul_mx(
-                                out=banks[n0, which][:, i, :],
-                                lhsT=lhsT,
-                                lhsT_scale=lhsT_scale,
-                                rhs=moving[a][0].bitcast(FP8X4),
-                                rhs_scale=moving[a][1],
-                                start=(a == 0 and i == 0),
-                                stop=(a == 1 and i == TILES_PER_BANK - 1),
-                            )
+                for bank, sums in zip(banks, BANK_SUMS):
+                    for i, (which, tile_n) in enumerate(sums):
+                        n = slice(tile_n * P, (tile_n + 1) * P)
+                        if which == 0:
+                            lhsT = w4_sb[:, a, 2 * n.start : 2 * n.stop].bitcast(FP4X4)
+                            lhsT_scale = w4_planes[:, a, n]
+                        else:
+                            lhsT = w5_codes[a][:, n].bitcast(FP8X4)
+                            lhsT_scale = w5_planes[a][:, n]
+                        nc.tensor.matmul_mx(
+                            out=bank[:, i, :],
+                            lhsT=lhsT,
+                            lhsT_scale=lhsT_scale,
+                            rhs=moving[a][0].bitcast(FP8X4),
+                            rhs_scale=moving[a][1],
+                            start=(a == 0 and i == 0),
+                            stop=(a == 1 and i == len(sums) - 1),
+                        )
             return banks
 
-        def higher(j0, banks):
-            for n0 in range(0, N // P, TILES_PER_BANK):
-                e1 = ring.tile([P, TILES_PER_BANK, TAIL], F32, name="e1")
-                nc.scalar.copy(e1[:], banks[n0, 0][:])
-                best = ring.tile([P, TILES_PER_BANK, TAIL], F32, name="best", bufs=4)
-                nc.vector.tensor_tensor(best[:], banks[n0, 1][:], e1[:], ALU.max)
+        def higher(c, banks):
+            j0 = c * CHUNK
+            for n0, count, e1_psum, e2_psum in (
+                (0, 4, banks[0][:], banks[1][:]),
+                (4, 2, banks[2][:, 0:2, :], banks[2][:, 2:4, :]),
+            ):
+                e1 = ring.tile([P, count, CHUNK], F32, name="e1")
+                nc.scalar.copy(e1[:], e1_psum)
+                best = ring.tile([P, count, CHUNK], F32, name="best", bufs=4)
+                nc.vector.tensor_tensor(best[:], e2_psum, e1[:], ALU.max)
                 nc.sync.dma_start(
-                    out[n0 * P : (n0 + TILES_PER_BANK) * P, j0 : j0 + TAIL].rearrange("(i p) j -> p i j", p=P),
+                    out[n0 * P : (n0 + count) * P, j0 : j0 + CHUNK].rearrange("(i p) j -> p i j", p=P),
                     best[:],
                 )
 
-        chunks = list(range(0, KEPT, TAIL))
-        rounded_a2, open_banks = {}, {}
-        for step in range(len(chunks) + 2):
-            if step < len(chunks):
-                j0 = chunks[step]
-                rounded_a2[j0] = ring.tile([P, TAIL, PACK], BF16, name="a2_high", align_bytes=64, bufs=4)
-                for t in range(PACK):
-                    kept(*high[t], 1, t, j0, TAIL, rounded_a2[j0])
-            if 1 <= step <= len(chunks):
-                j0 = chunks[step - 1]
-                open_banks[j0] = scores(j0, rounded_a2[j0])
+        chunks = KEPT // CHUNK
+        open_banks = []
+        finish_a2(PACK, 1)
+        finish_a2(SLICES - 1, 0)
+        for step in range(1, chunks + 2):
+            if step < chunks:
+                for s in range(PACK + (step == 1), SLICES):
+                    finish_a2(s, step)
+            if step <= chunks:
+                open_banks.append(scores(step - 1))
             if step >= 2:
-                j0 = chunks[step - 2]
-                higher(j0, open_banks[j0])
+                higher(step - 2, open_banks[step - 2])

@@ -1,6 +1,7 @@
 from contextlib import ExitStack
 
 import concourse.mybir as mybir
+from concourse.masks import make_identity
 
 K, T, S, H, N, PAIRS, KEPT = 1024, 4096, 2048, 1024, 768, 1024, 512
 FLOPS = 2 * K * H * S + 2 * 2 * H * N * KEPT
@@ -24,6 +25,7 @@ SLICES = H // P
 AHEAD = 3
 W5_PIECE = 384
 CHUNK = 128
+EARLY = 3
 BANK_SUMS = (
     ((0, 0), (0, 1), (0, 2), (0, 3)),
     ((1, 0), (1, 1), (1, 2), (1, 3)),
@@ -90,6 +92,8 @@ def tile_list_gravestone_inscription_scores_kernel(
                     picked_scales[a][32 * q : 32 * q + 4, :].bitcast(I32),
                     picked_rows[4 * row : 4 * row + 16 : 4, :].bitcast(I32),
                 )
+        identity = keep.tile([P, P], F32, name="identity")
+        make_identity(nc, identity[:])
         picked_low = mx_tile([P, S], U32, "picked_low")
         nc.vector.tensor_copy(picked_low[:], words[0][:].indirect(offs_sb[:]))
         picked = [[picked_low[:, c * BANK : (c + 1) * BANK] for c in range(S // BANK)], []]
@@ -117,7 +121,7 @@ def tile_list_gravestone_inscription_scores_kernel(
             )
 
         def rounded_tile(shape):
-            return ring.tile(shape, BF16, name="rounded", align_bytes=64)
+            return ring.tile(shape, BF16, name="rounded", align_bytes=64, bufs=3)
 
         w5_codes = [mx_tile([P, N], U32, "w5_codes%d" % a) for a in range(2)]
         w5_planes = [mx_tile([P, N], U8, "w5_planes%d" % a) for a in range(2)]
@@ -162,12 +166,30 @@ def tile_list_gravestone_inscription_scores_kernel(
                 both, a1[s][:].indirect(entries(pos3_sb, j0, width)), bounded[s][:, j0 : j0 + width], ALU.add
             )
 
+        def kept_sum_on_tensor(s, width, stronger):
+            bank = psum.tile([P, width], F32, name="bank")
+            for j0 in range(0, width, P):
+                for i, term in enumerate((stronger, bounded[s])):
+                    nc.tensor.matmul(
+                        bank[:, j0 : j0 + P],
+                        lhsT=term[:, j0 : j0 + P],
+                        rhs=identity[:],
+                        start=(i == 0),
+                        stop=(i == 1),
+                        is_transpose=True,
+                    )
+            turned = ring.tile([P, width], F32, name="turned")
+            nc.scalar.copy(turned[:], bank[:])
+            for j0 in range(0, width, P):
+                nc.tensor.transpose(bank[:, j0 : j0 + P], turned[:, j0 : j0 + P], identity[:])
+            return bank
+
         def round_a2(s, both, a2):
             b, t = divmod(s, PACK)
             nc.scalar.activation(a2[:, :, t], both, ACT.Copy, scale=gain_sb[:, b, t : t + 1])
 
-        def quantise_a2(a2, width, name):
-            codes = mx_tile([P, width], U32, name + "_codes")
+        def quantise_a2(a2, width, name, tag=None):
+            codes = mx_tile([P, width], U32, name + "_codes", tag)
             plane = mx_tile([P, width], U8, name + "_plane")
             nc.vector.quantize_mx(out=codes[:].bitcast(FP8X4), scales=plane[:], in_=a2[:].rearrange("p j t -> p (j t)"))
             return codes, plane
@@ -185,8 +207,8 @@ def tile_list_gravestone_inscription_scores_kernel(
             hs.append(features(s))
 
         for a in range(2):
-            w1_raw[a, 1] = load_rows(w1, a, K_PASS, K_PASS, "w1_raw%d1" % a, ("raw_even", "raw_odd")[a])
-        w5_raw = [load_rows(w5, a, 0, N, "w5_raw%d" % a, "words%d" % a) for a in range(2)]
+            w1_raw[a, 1] = load_rows(w1, a, K_PASS, K_PASS, "w1_raw%d1" % a, "words%d" % a)
+        w5_raw = [load_rows(w5, a, 0, N, "w5_raw%d" % a, ("raw_even", "raw_odd")[a]) for a in range(2)]
         w4_sb = mx_tile([P, 2, 2 * N], U8, "w4_sb", "picked_rows")
         nc.sync.dma_start(w4_sb[:].bitcast(I32), w4_words.rearrange("a p c -> p a c").bitcast(I32))
         w4_planes = mx_tile([P, 2, N], U8, "w4_planes")
@@ -201,43 +223,54 @@ def tile_list_gravestone_inscription_scores_kernel(
         a2_high = [mx_tile([P, CHUNK, PACK], BF16, "a2_high%d" % c) for c in range(KEPT // CHUNK)]
         a1, bounded = [], []
         half = PAIRS // 2
+        last = SLICES - 1
         for s in range(SLICES):
             h = hs[s]
-            entry = keep.tile([P, KEPT], F32, name="entry%d" % s, tag="entry%d" % s)
+            entry = mx_tile([P, KEPT], F32, "entry%d" % s)
             nc.vector.tensor_copy(entry[:], h[:].indirect(pos4_sb[:]))
             bounded.append(ring.tile([P, KEPT], F32, name="bounded", bufs=4))
             nc.scalar.activation(bounded[s][:], entry[:], ACT.Tanh)
-            first = ring.tile([P, PAIRS], F32, name="first")
+            if s == last - 1:
+                first = mx_tile([P, PAIRS], F32, "first%d" % s, "entry%d" % last)
+            else:
+                first = ring.tile([P, PAIRS], F32, name="first")
             nc.vector.tensor_copy(first[:], h[:].indirect(pos1_sb[:]))
-            if s > 0:
-                width = KEPT if s <= PACK else CHUNK
-                both = keep.tile([P, width], F32, name="both%d" % s, tag="entry%d" % s)
+            width = KEPT if s <= PACK else EARLY * CHUNK
+            if 0 < s < last:
+                stronger = mx_tile([P, width], F32, "stronger%d" % s, "entry%d" % s)
+                nc.vector.tensor_copy(stronger[:], a1[s - 1][:].indirect(entries(pos3_sb, 0, width)))
+            if s == last:
+                both = mx_tile([P, width], F32, "both%d" % s)
                 kept_sum(s - 1, 0, width, both[:])
-            second = keep.tile([P, PAIRS], F32, name="second%d" % s, tag="second")
-            for j0 in (0, half):
-                nc.vector.tensor_copy(second[:, j0 : j0 + half], h[:].indirect(entries(pos2_sb, j0, half)))
+            if s == last:
+                low_codes, low_plane = quantise_a2(a2_low, KEPT, "low", "entry%d" % last)
+            second = []
+            for i in range(2):
+                tag = "a2_low" if (s, i) == (last, 1) else "second%d" % i
+                second.append(mx_tile([P, half], F32, "second%d_%d" % (s, i), tag))
+                nc.vector.tensor_copy(second[i][:], h[:].indirect(entries(pos2_sb, i * half, half)))
             a1.append(ring.tile([P, PAIRS], F32, name="a1", bufs=4))
-            for j0 in (0, half):
-                cols = slice(j0, j0 + half)
-                nc.vector.tensor_tensor(a1[s][:, cols], first[:, cols], second[:, cols], ALU.max)
-            if s < 2:
-                quantise_w1(s, 1, 0, PACK, rounded_tile([P, PACK, P, PACK]))
-            if s > 0:
-                round_a2(s - 1, both[:], a2_low if s <= PACK else a2_high[0])
+            for i in range(2):
+                cols = slice(i * half, (i + 1) * half)
+                nc.vector.tensor_tensor(a1[s][:, cols], first[:, cols], second[i][:], ALU.max)
+            if s == 0:
+                for a in range(2):
+                    quantise_w1(a, 1, 0, PACK, rounded_tile([P, PACK, P, PACK]))
+            if 1 <= s <= 4:
+                quantise_w5((s - 1) // 2, (s - 1) % 2 * W5_PIECE)
             if s + AHEAD < SLICES:
                 hs.append(features(s + AHEAD))
-            if s == PACK + 1:
-                low_codes, low_plane = quantise_a2(a2_low, KEPT, "low")
-            if s in (PACK + 1, PACK + 2):
-                for c0 in range(0, N, W5_PIECE):
-                    quantise_w5(s - PACK - 1, c0)
+            if 0 < s < last:
+                both = kept_sum_on_tensor(s - 1, width, stronger)
+            if 0 < s <= PACK:
+                round_a2(s - 1, both[:], a2_low)
+            if s > PACK:
+                for c in range(EARLY):
+                    round_a2(s - 1, both[:, c * CHUNK : (c + 1) * CHUNK], a2_high[c])
 
-        late = keep.tile([P, KEPT * PACK], F32, name="late", tag="second")
-
-        def finish_a2(s, c):
-            at = (c * PACK + s - PACK) * CHUNK
-            kept_sum(s, c * CHUNK, CHUNK, late[:, at : at + CHUNK])
-            round_a2(s, late[:, at : at + CHUNK], a2_high[c])
+        def finish_a2(s, c, both):
+            kept_sum(s, c * CHUNK, CHUNK, both)
+            round_a2(s, both, a2_high[c])
 
         def scores(c):
             j0 = c * CHUNK
@@ -284,14 +317,14 @@ def tile_list_gravestone_inscription_scores_kernel(
                 )
 
         chunks = KEPT // CHUNK
-        open_banks = []
-        finish_a2(PACK, 1)
-        finish_a2(SLICES - 1, 0)
-        for step in range(1, chunks + 2):
-            if step < chunks:
-                for s in range(PACK + (step == 1), SLICES):
-                    finish_a2(s, step)
-            if step <= chunks:
-                open_banks.append(scores(step - 1))
-            if step >= 2:
-                higher(step - 2, open_banks[step - 2])
+        last_sums = mx_tile([P, EARLY, CHUNK], F32, "last_sums")
+        for c in range(EARLY):
+            finish_a2(last, c, last_sums[:, c, :])
+        open_banks = [scores(0)]
+        late_sums = mx_tile([P, PACK, CHUNK], F32, "late_sums", "a2_high0")
+        for t in range(PACK):
+            finish_a2(PACK + t, chunks - 1, late_sums[:, t, :])
+        for c in range(1, chunks):
+            open_banks.append(scores(c))
+            higher(c - 1, open_banks[c - 1])
+        higher(chunks - 1, open_banks[chunks - 1])

from contextlib import ExitStack

import concourse.mybir as mybir
from concourse.masks import make_identity

K, T, S, H, N, PAIRS, KEPT = 1024, 4096, 2048, 1024, 768, 1024, 512
FLOPS = 2 * K * H * S + 2 * 2 * H * N * KEPT

F32 = mybir.dt.float32
BF16 = mybir.dt.bfloat16
I32 = mybir.dt.int32
U32 = mybir.dt.uint32
U16 = mybir.dt.uint16
U8 = mybir.dt.uint8
FP8X4 = mybir.dt.float8_e4m3fn_x4
FP4X4 = mybir.dt.float4_e2m1fn_x4
ACT = mybir.ActivationFunctionType
ALU = mybir.AluOpType

P = 128
PACK = 4
K_PASS = P * PACK
BANK = 512
SLICES = H // P
AHEAD = 3
W5_PIECE = 384
CHUNK = 128
EARLY = 3
BANK_SUMS = (
    ((0, 0), (0, 1), (0, 2), (0, 3)),
    ((1, 0), (1, 1), (1, 2), (1, 3)),
    ((0, 4), (0, 5), (1, 4), (1, 5)),
)


def tile_list_gravestone_inscription_scores_kernel(
    tc, tab_words, tab_scales, offs, pos1, pos2, pos3, pos4, w1, gain, w4_words, w4_scales, w5, out
):
    nc = tc.nc
    with ExitStack() as ctx:
        keep = ctx.enter_context(tc.tile_pool(name="keep", bufs=1))
        ring = ctx.enter_context(tc.tile_pool(name="ring", bufs=2))
        psum = ctx.enter_context(tc.psum_pool(name="psum", bufs=8))

        def mx_tile(shape, dtype, name, tag=None):
            return keep.tile(shape, dtype, name=name, tag=tag or name, align_bytes=64)

        def load_list(src, name):
            t = keep.tile(list(src.shape), U16, name=name)
            nc.sync.dma_start(t[:], src)
            return t

        def load_rows(w, a, c0, width, name, tag):
            raw = mx_tile([P, PACK, width], F32, name, tag)
            nc.sync.dma_start(
                raw[:], w[a * K_PASS : (a + 1) * K_PASS, c0 : c0 + width].rearrange("(p j) c -> p j c", j=PACK)
            )
            return raw

        def entries(lst, j0, count):
            return lst[:, j0 // 16 : (j0 + count) // 16]

        offs_sb = load_list(offs, "offs_sb")
        scale_rows = mx_tile([P, T], U8, "scale_rows")
        nc.sync.dma_start(
            scale_rows[:].bitcast(I32),
            tab_scales.rearrange("a q t -> (a q) t").bitcast(I32).unsqueeze(1).to_broadcast([32, 4, T // 4]),
        )
        pos4_sb = load_list(pos4, "pos4_sb")
        pos1_sb = load_list(pos1, "pos1_sb")
        pos2_sb = load_list(pos2, "pos2_sb")
        pos3_sb = load_list(pos3, "pos3_sb")
        words = []
        for a in range(2):
            t = mx_tile([P, T], U32, "words%d" % a)
            nc.sync.dma_start(t[:].bitcast(I32), tab_words[a].rearrange("p t i -> p (t i)").bitcast(I32))
            words.append(t)
        w1_raw = {}
        for a in range(2):
            w1_raw[a, 0] = load_rows(w1, a, 0, K_PASS, "w1_raw%d0" % a, ("raw_even", "raw_odd")[a])
        gain_sb = keep.tile([P, 2, PACK], F32, name="gain_sb")
        nc.sync.dma_start(gain_sb[:], gain.rearrange("(b p t) -> p b t", b=2, t=PACK))

        picked_rows = mx_tile([P, S], U8, "picked_rows")
        nc.vector.tensor_copy(picked_rows[:], scale_rows[:].indirect(offs_sb[:]))
        picked_scales = [mx_tile([P, S], U8, "picked_scales%d" % a) for a in range(2)]
        for a in range(2):
            nc.gpsimd.memset(picked_scales[a][:].bitcast(I32), 0)
            for q in range(4):
                row = 16 * a + 4 * q
                (nc.scalar, nc.sync)[a].dma_start(
                    picked_scales[a][32 * q : 32 * q + 4, :].bitcast(I32),
                    picked_rows[4 * row : 4 * row + 16 : 4, :].bitcast(I32),
                )
        identity = keep.tile([P, P], F32, name="identity")
        make_identity(nc, identity[:])
        picked_low = mx_tile([P, S], U32, "picked_low")
        nc.vector.tensor_copy(picked_low[:], words[0][:].indirect(offs_sb[:]))
        picked = [[picked_low[:, c * BANK : (c + 1) * BANK] for c in range(S // BANK)], []]

        def pick_high(c):
            t = mx_tile([P, BANK], U32, "picked_high%d" % c)
            nc.vector.tensor_copy(t[:], words[1][:].indirect(entries(offs_sb, c * BANK, BANK)))
            picked[1].append(t[:])

        w1_codes, w1_planes = {}, {}
        for a in range(2):
            for b in range(2):
                w1_codes[a, b] = mx_tile([P, K_PASS], U32, "w1_codes%d%d" % (a, b))
                w1_planes[a, b] = mx_tile([P, K_PASS], U8, "w1_planes%d%d" % (a, b))

        def quantise_w1(a, b, t0, t1, rounded):
            nc.scalar.copy(
                rounded[:].rearrange("p t m j -> p m j t"),
                w1_raw[a, b][:].rearrange("p j (m t) -> p m j t", t=PACK)[:, :, :, t0:t1],
            )
            nc.vector.quantize_mx(
                out=w1_codes[a, b][:, t0 * P : t1 * P].bitcast(FP8X4),
                scales=w1_planes[a, b][:, t0 * P : t1 * P],
                in_=rounded[:].rearrange("p t m j -> p (t m j)"),
            )

        def rounded_tile(shape):
            return ring.tile(shape, BF16, name="rounded", align_bytes=64, bufs=3)

        w5_codes = [mx_tile([P, N], U32, "w5_codes%d" % a) for a in range(2)]
        w5_planes = [mx_tile([P, N], U8, "w5_planes%d" % a) for a in range(2)]

        def quantise_w5(a, c0):
            rounded = rounded_tile([P, W5_PIECE, PACK])
            nc.scalar.copy(
                rounded[:].rearrange("p (c i) j -> p c j i", i=4),
                w5_raw[a][:, :, c0 : c0 + W5_PIECE].rearrange("p j (c i) -> p c j i", i=4),
            )
            nc.vector.quantize_mx(
                out=w5_codes[a][:, c0 : c0 + W5_PIECE].bitcast(FP8X4),
                scales=w5_planes[a][:, c0 : c0 + W5_PIECE],
                in_=rounded[:].rearrange("p c j -> p (c j)"),
            )

        def features(s):
            b, t = divmod(s, PACK)
            h = ring.tile([P, S], F32, name="h", bufs=AHEAD)
            m = slice(t * P, (t + 1) * P)
            for c in range(S // BANK):
                cols = slice(c * BANK, (c + 1) * BANK)
                acc = psum.tile([P, BANK], F32, name="bank")
                for a in range(2):
                    nc.tensor.matmul_mx(
                        out=acc[:],
                        lhsT=w1_codes[a, b][:, m].bitcast(FP8X4),
                        lhsT_scale=w1_planes[a, b][:, m],
                        rhs=picked[a][c].bitcast(FP8X4),
                        rhs_scale=picked_scales[a][:, cols],
                        start=(a == 0),
                        stop=(a == 1),
                    )
                if s == 0:
                    nc.vector.tensor_copy(h[:, cols], acc[:])
                else:
                    nc.scalar.copy(h[:, cols], acc[:])
            return h

        def kept_sum(s, j0, width, both):
            nc.vector.tensor_tensor(
                both, a1[s][:].indirect(entries(pos3_sb, j0, width)), bounded[s][:, j0 : j0 + width], ALU.add
            )

        def kept_sum_on_tensor(s, width, stronger):
            bank = psum.tile([P, width], F32, name="bank")
            for j0 in range(0, width, P):
                for i, term in enumerate((stronger, bounded[s])):
                    nc.tensor.matmul(
                        bank[:, j0 : j0 + P],
                        lhsT=term[:, j0 : j0 + P],
                        rhs=identity[:],
                        start=(i == 0),
                        stop=(i == 1),
                        is_transpose=True,
                    )
            turned = ring.tile([P, width], F32, name="turned")
            nc.scalar.copy(turned[:], bank[:])
            for j0 in range(0, width, P):
                nc.tensor.transpose(bank[:, j0 : j0 + P], turned[:, j0 : j0 + P], identity[:])
            return bank

        def round_a2(s, both, a2):
            b, t = divmod(s, PACK)
            nc.scalar.activation(a2[:, :, t], both, ACT.Copy, scale=gain_sb[:, b, t : t + 1])

        def quantise_a2(a2, width, name, tag=None):
            codes = mx_tile([P, width], U32, name + "_codes", tag)
            plane = mx_tile([P, width], U8, name + "_plane")
            nc.vector.quantize_mx(out=codes[:].bitcast(FP8X4), scales=plane[:], in_=a2[:].rearrange("p j t -> p (j t)"))
            return codes, plane

        pick_high(0)
        pick_high(1)
        quantise_w1(0, 0, 0, 1, mx_tile([P, 1, P, PACK], BF16, "first_rounded", "picked_high2"))
        pick_high(2)
        pick_high(3)
        quantise_w1(1, 0, 0, 1, mx_tile([P, 1, P, PACK], BF16, "second_rounded", "w4_planes"))
        hs = [features(0)]
        quantise_w1(0, 0, 1, PACK, mx_tile([P, PACK - 1, P, PACK], BF16, "third_rounded", "w4_planes"))
        quantise_w1(1, 0, 1, PACK, rounded_tile([P, PACK - 1, P, PACK]))
        for s in range(1, AHEAD):
            hs.append(features(s))

        for a in range(2):
            w1_raw[a, 1] = load_rows(w1, a, K_PASS, K_PASS, "w1_raw%d1" % a, "words%d" % a)
        w5_raw = [load_rows(w5, a, 0, N, "w5_raw%d" % a, ("raw_even", "raw_odd")[a]) for a in range(2)]
        w4_sb = mx_tile([P, 2, 2 * N], U8, "w4_sb", "picked_rows")
        nc.sync.dma_start(w4_sb[:].bitcast(I32), w4_words.rearrange("a p c -> p a c").bitcast(I32))
        w4_planes = mx_tile([P, 2, N], U8, "w4_planes")
        nc.gpsimd.memset(w4_planes[:].bitcast(I32), 0)
        for q in range(4):
            nc.sync.dma_start(
                w4_planes[32 * q : 32 * q + 4, :, :].bitcast(I32),
                w4_scales[:, 4 * q : 4 * q + 4, :].rearrange("a r c -> r a c").bitcast(I32),
            )

        a2_low = mx_tile([P, KEPT, PACK], BF16, "a2_low")
        a2_high = [mx_tile([P, CHUNK, PACK], BF16, "a2_high%d" % c) for c in range(KEPT // CHUNK)]
        a1, bounded = [], []
        half = PAIRS // 2
        last = SLICES - 1
        for s in range(SLICES):
            h = hs[s]
            entry = mx_tile([P, KEPT], F32, "entry%d" % s)
            nc.vector.tensor_copy(entry[:], h[:].indirect(pos4_sb[:]))
            bounded.append(ring.tile([P, KEPT], F32, name="bounded", bufs=4))
            nc.scalar.activation(bounded[s][:], entry[:], ACT.Tanh)
            if s == last - 1:
                first = mx_tile([P, PAIRS], F32, "first%d" % s, "entry%d" % last)
            else:
                first = ring.tile([P, PAIRS], F32, name="first")
            nc.vector.tensor_copy(first[:], h[:].indirect(pos1_sb[:]))
            width = KEPT if s <= PACK else EARLY * CHUNK
            if 0 < s < last:
                stronger = mx_tile([P, width], F32, "stronger%d" % s, "entry%d" % s)
                nc.vector.tensor_copy(stronger[:], a1[s - 1][:].indirect(entries(pos3_sb, 0, width)))
            if s == last:
                both = mx_tile([P, width], F32, "both%d" % s)
                kept_sum(s - 1, 0, width, both[:])
            if s == last:
                low_codes, low_plane = quantise_a2(a2_low, KEPT, "low", "entry%d" % last)
            second = []
            for i in range(2):
                tag = "a2_low" if (s, i) == (last, 1) else "second%d" % i
                second.append(mx_tile([P, half], F32, "second%d_%d" % (s, i), tag))
                nc.vector.tensor_copy(second[i][:], h[:].indirect(entries(pos2_sb, i * half, half)))
            a1.append(ring.tile([P, PAIRS], F32, name="a1", bufs=4))
            for i in range(2):
                cols = slice(i * half, (i + 1) * half)
                nc.vector.tensor_tensor(a1[s][:, cols], first[:, cols], second[i][:], ALU.max)
            if s == 0:
                for a in range(2):
                    quantise_w1(a, 1, 0, PACK, rounded_tile([P, PACK, P, PACK]))
            if 1 <= s <= 4:
                quantise_w5((s - 1) // 2, (s - 1) % 2 * W5_PIECE)
            if s + AHEAD < SLICES:
                hs.append(features(s + AHEAD))
            if 0 < s < last:
                both = kept_sum_on_tensor(s - 1, width, stronger)
            if 0 < s <= PACK:
                round_a2(s - 1, both[:], a2_low)
            if s > PACK:
                for c in range(EARLY):
                    round_a2(s - 1, both[:, c * CHUNK : (c + 1) * CHUNK], a2_high[c])

        def finish_a2(s, c, both):
            kept_sum(s, c * CHUNK, CHUNK, both)
            round_a2(s, both, a2_high[c])

        def scores(c):
            j0 = c * CHUNK
            high_codes, high_plane = quantise_a2(a2_high[c], CHUNK, "high%d" % c)
            moving = [
                (low_codes[:, j0 : j0 + CHUNK], low_plane[:, j0 : j0 + CHUNK]),
                (high_codes[:], high_plane[:]),
            ]
            banks = [psum.tile([P, PACK, CHUNK], F32, name="bank") for sums in BANK_SUMS]
            for a in range(2):
                for bank, sums in zip(banks, BANK_SUMS):
                    for i, (which, tile_n) in enumerate(sums):
                        n = slice(tile_n * P, (tile_n + 1) * P)
                        if which == 0:
                            lhsT = w4_sb[:, a, 2 * n.start : 2 * n.stop].bitcast(FP4X4)
                            lhsT_scale = w4_planes[:, a, n]
                        else:
                            lhsT = w5_codes[a][:, n].bitcast(FP8X4)
                            lhsT_scale = w5_planes[a][:, n]
                        nc.tensor.matmul_mx(
                            out=bank[:, i, :],
                            lhsT=lhsT,
                            lhsT_scale=lhsT_scale,
                            rhs=moving[a][0].bitcast(FP8X4),
                            rhs_scale=moving[a][1],
                            start=(a == 0 and i == 0),
                            stop=(a == 1 and i == len(sums) - 1),
                        )
            return banks

        def higher(c, banks):
            j0 = c * CHUNK
            for n0, count, e1_psum, e2_psum in (
                (0, 4, banks[0][:], banks[1][:]),
                (4, 2, banks[2][:, 0:2, :], banks[2][:, 2:4, :]),
            ):
                e1 = ring.tile([P, count, CHUNK], F32, name="e1")
                nc.scalar.copy(e1[:], e1_psum)
                best = ring.tile([P, count, CHUNK], F32, name="best", bufs=4)
                nc.vector.tensor_tensor(best[:], e2_psum, e1[:], ALU.max)
                nc.sync.dma_start(
                    out[n0 * P : (n0 + count) * P, j0 : j0 + CHUNK].rearrange("(i p) j -> p i j", p=P),
                    best[:],
                )

        chunks = KEPT // CHUNK
        last_sums = mx_tile([P, EARLY, CHUNK], F32, "last_sums")
        for c in range(EARLY):
            finish_a2(last, c, last_sums[:, c, :])
        open_banks = [scores(0)]
        late_sums = mx_tile([P, PACK, CHUNK], F32, "late_sums", "a2_high0")
        for t in range(PACK):
            finish_a2(PACK + t, chunks - 1, late_sums[:, t, :])
        for c in range(1, chunks):
            open_banks.append(scores(c))
            higher(c - 1, open_banks[c - 1])
        higher(chunks - 1, open_banks[chunks - 1])
